import numpy as np
import ml_dtypes


def mxq(x, axis, fmt="e4m3"):
    dtype, down = {"e4m3": (ml_dtypes.float8_e4m3fn, 7), "e5m2": (ml_dtypes.float8_e5m2, 14)}[fmt]
    v = np.moveaxis(np.asarray(x, np.float32).astype(ml_dtypes.bfloat16).astype(np.float64), axis, -1)
    blocks = v.reshape(v.shape[:-1] + (-1, 32))
    amax = np.abs(blocks).max(-1, keepdims=True)
    byte = np.maximum(np.where(amax > 0, np.frexp(amax)[1] - 1 + 127, 0) - down, 1)
    scale = np.exp2(byte - 127.0)
    codes = (blocks / scale).astype(np.float32).astype(dtype).astype(np.float64)
    return np.moveaxis((codes * scale).reshape(v.shape), -1, axis)


WIDE = False


def mx_kscale(k):
    if not WIDE:
        return np.ones(k)
    levels = np.array([10, -10, 5, -5, 0])
    if k % 512:
        return np.exp2(np.random.permutation(np.resize(levels, k // 32))).repeat(32)
    a = np.empty((k // 512, 16))
    for p in range(k // 512):
        a[p, :8] = np.random.permutation(np.resize(levels, 8))
        for g in range(8):
            far = levels[np.abs(levels - a[p, g]) >= 10]
            a[p, g + 8] = far[np.random.randint(len(far))]
    return np.exp2(a.ravel()).repeat(32)


def f64(x):
    return np.asarray(x).astype(np.float64)


def striped(idx):
    return np.tile(idx.reshape(-1, 16).T, (8, 1)).astype(np.uint16)


def unstriped(offs):
    return offs[:16].T.reshape(-1).astype(np.int64)


def striped8(idx):
    return np.concatenate([x.reshape(-1, 16).T for x in idx]).astype(np.uint16)


def runs(offs, k):
    lists = np.stack([offs[16 * r : 16 * r + 16].T.reshape(-1) for r in range(8)]).astype(np.int64)
    return lists[np.arange(k) % 512 // 64]


def pack_weight(w):
    k, n = w.shape
    w = f64(np.asarray(w, np.float32).astype(ml_dtypes.bfloat16)).reshape(k // 32, 32, n)
    amax = np.abs(w).max(1)
    byte = np.clip(np.where(amax > 0, np.frexp(amax)[1] - 1 + 127 - 7, 1), 1, 254)
    scaled = (w * np.exp2(127.0 - byte)[:, None, :]).reshape(k, n).astype(np.float32)
    words = np.ascontiguousarray(scaled.reshape(k // 512, 128, 4, n).transpose(0, 1, 3, 2)).astype(ml_dtypes.float8_e4m3fn).view(np.uint8)
    return words, np.ascontiguousarray(byte.astype(np.uint8).reshape(k // 512, 16, n))


def unpack_weight(words, scales):
    g, p, n, _ = words.shape
    vals = np.ascontiguousarray(words).view(ml_dtypes.float8_e4m3fn).astype(np.float64) * np.repeat(np.exp2(scales.astype(np.float64) - 127.0), 8, axis=1)[..., None]
    return vals.transpose(0, 1, 3, 2).reshape(g * 512, n)


K, T, S, V, H, W = 512, 2048, 512, 512, 512, 256


def setup_inputs():
    n = np.random.standard_normal
    s = mx_kscale(K)[:, None]
    u = mx_kscale(S)
    packed_xT = pack_weight(n((K, T)) * s)
    perm = np.stack([np.random.permutation(V) for _ in range(8)])
    return {
        "x_words": packed_xT[0],
        "x_scales": packed_xT[1],
        "w1": (n((K, H)) / np.sqrt(K) / s).astype(np.float32),
        "w2": (n((K, H)) / np.sqrt(K) / s).astype(np.float32),
        "w3": (n((K, H)) / np.sqrt(K) / s).astype(np.float32),
        "ga": (np.random.uniform(0.5, 1.5, (H, 1)) * u[:, None]).astype(np.float32),
        "gb": (np.random.uniform(0.5, 1.5, (H, 1)) / u[:, None]).astype(np.float32),
        "offs": striped(np.random.permutation(T)[:S]),
        "two": striped(np.random.permutation(T)[:S]),
        "n1": striped8(np.stack([np.random.permutation(S) for _ in range(8)])),
        "n2": striped8(np.stack([np.random.permutation(S) for _ in range(8)])),
        "three": striped(np.random.permutation(T)[:V]),
        "n3": striped8(perm[:, :W]),
        "n4": striped8(perm[:, W:]),
        "n5": striped8(np.stack([np.random.permutation(V) for _ in range(8)])),
        "n6": striped8(np.stack([np.random.permutation(V) for _ in range(8)])),
    }


def reference(x_words, x_scales, w1, w2, w3, ga, gb, offs, two, n1, n2, three, n3, n4, n5, n6):
    xq = unpack_weight(x_words, x_scales)[:, unstriped(offs)]
    y = mxq(f64(w1), 0, "e4m3").T @ xq
    x_two = unpack_weight(x_words, x_scales)[:, unstriped(two)]
    d = mxq(f64(w2), 0, "e4m3").T @ x_two
    z = f64(ga) * ((y - (y[np.arange(H)[:, None], runs(n1, H)])) / (np.abs(d) + np.abs(d[np.arange(H)[:, None], runs(n2, H)]) + 0.5))
    x_three = unpack_weight(x_words, x_scales)[:, unstriped(three)]
    b = mxq(f64(w3), 0, "e4m3").T @ x_three
    pa = b[np.arange(H)[:, None], runs(n3, H)]
    pb = b[np.arange(H)[:, None], runs(n4, H)]
    rb = pa - pb
    ra = 0.75 * (pa + pb)
    ds = np.zeros((H, V))
    ds[np.arange(H)[:, None], runs(n3, H)] = ra
    dt = ds.copy()
    dt[np.arange(H)[:, None], runs(n4, H)] = rb
    z2 = f64(gb) * dt
    s = 0.0625 * ((mxq(z, 0, "e4m3").T @ mxq(z2, 0, "e4m3")))
    return (s[np.arange(S)[:, None], runs(n5, S)]) * (s[np.arange(S)[:, None], runs(n6, S)])

@@ -1,0 +1,210 @@
+from contextlib import ExitStack
+
+import concourse.mybir as mybir
+from concourse.masks import make_identity
+
+K, T, S, V, H, W = 512, 2048, 512, 512, 512, 256
+FLOPS = 4 * 2 * 512 * 512 * 512
+
+F32 = mybir.dt.float32
+BF16 = mybir.dt.bfloat16
+I32 = mybir.dt.int32
+U32 = mybir.dt.uint32
+U16 = mybir.dt.uint16
+U8 = mybir.dt.uint8
+FP8X4 = mybir.dt.float8_e4m3fn_x4
+ALU = mybir.AluOpType
+ACT = mybir.ActivationFunctionType
+P = 128
+
+
+def tile_picked_twknormbhaarprod_none_p_kernel(tc, x_words, x_scales, w1, w2, w3, ga, gb, offs, two, n1, n2, three, n3, n4, n5, n6, out):
+    nc = tc.nc
+    with ExitStack() as ctx:
+        held = ctx.enter_context(tc.tile_pool(name="held", bufs=1))
+        psum = ctx.enter_context(tc.psum_pool(name="psum", bufs=8))
+
+        def sb(name, shape, dtype):
+            return held.tile(shape, dtype, name=name, align_bytes=64)
+
+        lists = {}
+
+        def load_list(name, src):
+            lists[name] = sb("list_" + name, list(src.shape), U16)
+            nc.sync.dma_start(lists[name][:], src)
+
+        def load_w(name, src):
+            raw = sb(name + "_raw", [P, 4, H], F32)
+            nc.sync.dma_start(raw[:], src.rearrange("(p j) c -> p j c", j=4))
+            return raw
+
+        xs = sb("xs", [P, T], U8)
+        nc.vector.memset(xs[:].bitcast(I32), 0)
+        for q in range(4):
+            nc.scalar.dma_start(xs[32 * q : 32 * q + 4, :].bitcast(I32), x_scales[0, 4 * q : 4 * q + 4, :].bitcast(I32))
+        load_list("three", three)
+        w3_raw = load_w("w3", w3)
+        xw = sb("xw", [P, T], I32)
+        nc.sync.dma_start(xw[:], x_words[0].rearrange("p n t -> p (n t)").bitcast(I32))
+        load_list("offs", offs)
+        load_list("two", two)
+        load_list("n3", n3)
+        load_list("n4", n4)
+        w1_raw = load_w("w1", w1)
+        w2_raw = load_w("w2", w2)
+        for name, src in (("n1", n1), ("n2", n2), ("n5", n5), ("n6", n6)):
+            load_list(name, src)
+        ident = sb("ident", [P, P], F32)
+        make_identity(nc, ident[:])
+        gain_rows = sb("gain_rows", [P, P], F32)
+        nc.vector.memset(gain_rows[:], 0.0)
+        nc.scalar.dma_start(gain_rows[0:4, :].rearrange("t (b q) -> t b q", q=8), gb.rearrange("(b t q) o -> t b (q o)", t=4, q=8))
+        nc.scalar.dma_start(gain_rows[4:8, :].rearrange("t (b q) -> t b q", q=8), ga.rearrange("(b t q) o -> t b (q o)", t=4, q=8))
+        gain_acc = psum.tile([P, 512], F32, name="acc")
+        nc.tensor.transpose(gain_acc[:, 0:P], gain_rows[:], ident[:])
+        gains = sb("gains", [P, 8], F32)
+        nc.scalar.copy(gains[:], gain_acc[:, 0:8])
+        three_quarters = sb("three_quarters", [P, W], F32)
+        nc.gpsimd.memset(three_quarters[:], 0.75)
+
+        picked_scales = {}
+        picked_words = {}
+
+        def pick_scales(name):
+            picked_scales[name] = sb("ps_" + name, [P, S], U8)
+            nc.vector.tensor_copy(picked_scales[name][:], xs[:].indirect(lists[name][:]))
+
+        def pick_words(name):
+            picked_words[name] = sb("pw_" + name, [P, S], U32)
+            nc.vector.tensor_copy(picked_words[name][:], xw[:].bitcast(U32).indirect(lists[name][:]))
+
+        def cast_w(name, raw):
+            tiles = []
+            for t in range(4):
+                g = sb(name + "_g%d" % t, [P, 4 * P], BF16)
+                nc.scalar.copy(
+                    g[:].rearrange("p (b a i j) -> p b a j i", a=2, i=4, j=4),
+                    raw[:].rearrange("p j (b t a i) -> p t b a j i", t=4, a=2, i=4)[:, t],
+                )
+                tiles.append(g)
+            return tiles
+
+        def quant_w(name, tiles):
+            res = []
+            for t in range(4):
+                c = sb(name + "_c%d" % t, [P, P], U32)
+                s = sb(name + "_s%d" % t, [P, P], U8)
+                nc.vector.quantize_mx(c[:].bitcast(FP8X4), s[:], tiles[t][:])
+                res.append((c, s))
+            return res
+
+        def product(lc, ls, rc, rs):
+            acc = psum.tile([P, 512], F32, name="acc")
+            nc.tensor.matmul_mx(acc[:], lhsT=lc.bitcast(FP8X4), lhsT_scale=ls, rhs=rc.bitcast(FP8X4), rhs_scale=rs, start=True, stop=True)
+            return acc
+
+        def project(wq, name):
+            return [product(c[:], s[:], picked_words[name][:], picked_scales[name][:]) for c, s in wq]
+
+        for name in ("three", "offs", "two"):
+            pick_scales(name)
+        w3_g = cast_w("w3", w3_raw)
+        pick_words("three")
+        b_acc = project(quant_w("w3", w3_g), "three")
+        pick_words("offs")
+        pick_words("two")
+
+        z2_rows = sb("z2_rows", [P, 4, V], F32)
+
+        def haar(t):
+            win = sb("b%d" % t, [P, V], F32)
+            nc.scalar.activation(win[:], b_acc[t][:], ACT.Copy, scale=gains[:, t : t + 1])
+            pa = sb("pa%d" % t, [P, W], F32)
+            npb = sb("npb%d" % t, [P, W], F32)
+            nc.scalar.activation(pa[:], win[:].indirect(lists["n3"][:]), ACT.Copy)
+            nc.scalar.activation(npb[:], win[:].indirect(lists["n4"][:]), ACT.Copy, scale=-1.0)
+            both = sb("both%d" % t, [P, W], F32)
+            dt = sb("dt%d" % t, [P, V], F32)
+            nc.vector.tensor_tensor(both[:], pa[:], npb[:], ALU.subtract)
+            nc.vector.tensor_tensor(dt[:].indirect(lists["n4"][:]), pa[:], npb[:], ALU.add)
+            nc.vector.tensor_tensor(dt[:].indirect(lists["n3"][:]), both[:], three_quarters[:], ALU.mult)
+            if t < 3:
+                nc.sync.dma_start(z2_rows[:, t, :], dt[:])
+            else:
+                nc.vector.tensor_copy(z2_rows[:, t, :], dt[:])
+
+        haar(0)
+        y_acc = project(quant_w("w1", cast_w("w1", w1_raw)), "offs")
+        haar(1)
+        d_acc = project(quant_w("w2", cast_w("w2", w2_raw)), "two")
+        haar(2)
+        haar(3)
+
+        yw = []
+        dw = []
+        for t in range(4):
+            yw.append(sb("y%d" % t, [P, S], F32))
+            nc.scalar.activation(yw[t][:], y_acc[t][:], ACT.Copy, scale=gains[:, 4 + t : 5 + t])
+        for t in range(4):
+            dw.append(sb("d%d" % t, [P, S], F32))
+            nc.scalar.activation(dw[t][:], d_acc[t][:], ACT.Abs)
+
+        z2_g = sb("z2_g", [P, 4 * V], BF16)
+        nc.vector.tensor_copy(
+            z2_g[:].rearrange("p (c i t) -> p c t i", i=4, t=4),
+            z2_rows[:].rearrange("p t (c i) -> p c t i", i=4),
+        )
+        z2_c = sb("z2_c", [P, V], U32)
+        z2_s = sb("z2_s", [P, V], U8)
+        nc.vector.quantize_mx(z2_c[:].bitcast(FP8X4), z2_s[:], z2_g[:])
+
+        z_c = sb("z_c", [P, S], U32)
+        z_s = sb("z_s", [P, S], U8)
+        for h in range(2):
+            cols = slice(256 * h, 256 * h + 256)
+            lcols = slice(16 * h, 16 * h + 16)
+            num = sb("num%d" % h, [P, 4, 256], F32)
+            den = sb("den%d" % h, [P, 4, 256], F32)
+            for wins, lst, res, op in ((dw, "n2", den, ALU.add), (yw, "n1", num, ALU.subtract)):
+                for t in range(4):
+                    got = sb("got_%s_%d_%d" % (lst, h, t), [P, 256], F32)
+                    nc.scalar.activation(got[:], wins[t][:].indirect(lists[lst][:, lcols]), ACT.Copy)
+                    nc.vector.tensor_tensor(
+                        res[:, t, :].rearrange("p (m g q) -> p g m q", m=4, g=8),
+                        wins[t][:, cols].rearrange("p (g m q) -> p g m q", m=4, g=8),
+                        got[:].rearrange("p (g m q) -> p g m q", m=4, g=8),
+                        op,
+                    )
+            root = sb("root%d" % h, [P, 4 * 256], F32)
+            nc.scalar.activation(root[:], den[:].rearrange("p t c -> p (t c)"), ACT.Abs_reciprocal_sqrt, bias=0.5)
+            part = sb("part%d" % h, [P, 4 * 256], F32)
+            nc.vector.tensor_tensor(part[:], num[:].rearrange("p t c -> p (t c)"), root[:], ALU.mult)
+            z_g = sb("z_g%d" % h, [P, 4 * 256], BF16)
+            nc.vector.tensor_tensor(
+                z_g[:].rearrange("p (c i t) -> p c t i", i=4, t=4),
+                part[:].rearrange("p (t c i) -> p c t i", t=4, i=4),
+                root[:].rearrange("p (t c i) -> p c t i", t=4, i=4),
+                ALU.mult,
+            )
+            for m in range(4):
+                at = slice(P * m + 64 * h, P * m + 64 * h + 64)
+                nc.vector.quantize_mx(z_c[:, at].bitcast(FP8X4), z_s[:, at], z_g[:, 256 * m : 256 * m + 256])
+
+        rows = out.rearrange("(g m q) v -> m g q v", m=4, q=8)
+        s_acc = [product(z_c[:, P * m : P * m + P], z_s[:, P * m : P * m + P], z2_c[:], z2_s[:]) for m in range(4)]
+        sw = []
+        for m in range(4):
+            sw.append(sb("s%d" % m, [P, V], F32))
+            if m in (0, 3):
+                nc.scalar.activation(sw[m][:], s_acc[m][:], ACT.Copy, scale=0.0625)
+            else:
+                nc.vector.tensor_scalar(sw[m][:], s_acc[m][:], 0.0625, None, ALU.mult)
+        for m in range(4):
+            res = sb("res%d" % m, [P, V], F32)
+            for h in range(2):
+                cols = slice(256 * h, 256 * h + 256)
+                lcols = slice(16 * h, 16 * h + 16)
+                first = sb("first%d_%d" % (m, h), [P, 256], F32)
+                nc.scalar.activation(first[:], sw[m][:].indirect(lists["n5"][:, lcols]), ACT.Copy)
+                nc.vector.tensor_tensor(res[:, cols], sw[m][:].indirect(lists["n6"][:, lcols]), first[:], ALU.mult)
+            nc.sync.dma_start(rows[m], res[:])

@@ -22,10 +22,13 @@ def tile_picked_twknormbhaarprod_none_p_kernel(tc, x_words, x_scales, w1, w2, w3
     nc = tc.nc
     with ExitStack() as ctx:
         held = ctx.enter_context(tc.tile_pool(name="held", bufs=1))
-        psum = ctx.enter_context(tc.psum_pool(name="psum", bufs=8))
+        psum = ctx.enter_context(tc.psum_pool(name="psum", bufs=1))
 
-        def sb(name, shape, dtype):
-            return held.tile(shape, dtype, name=name, align_bytes=64)
+        def sb(name, shape, dtype, tag=None):
+            return held.tile(shape, dtype, name=name, tag=tag or name, align_bytes=64)
+
+        def bank(name, number):
+            return psum.tile([P, 512], F32, name=name, tag="bank%d" % number)
 
         lists = {}
 
@@ -38,16 +41,20 @@ def tile_picked_twknormbhaarprod_none_p_kernel(tc, x_words, x_scales, w1, w2, w3
             nc.sync.dma_start(raw[:], src.rearrange("(p j) c -> p j c", j=4))
             return raw
 
+        gain_rows = sb("gain_rows", [P, P], F32)
+        nc.gpsimd.memset(gain_rows[:], 0.0)
         xs = sb("xs", [P, T], U8)
-        nc.vector.memset(xs[:].bitcast(I32), 0)
-        for q in range(4):
-            nc.scalar.dma_start(xs[32 * q : 32 * q + 4, :].bitcast(I32), x_scales[0, 4 * q : 4 * q + 4, :].bitcast(I32))
         load_list("three", three)
+        for q in range(4):
+            rows4 = x_scales[0, 4 * q : 4 * q + 4, :].bitcast(I32)
+            nc.sync.dma_start(xs[32 * q : 32 * q + 32, :].bitcast(I32), rows4.unsqueeze(0).to_broadcast([8, 4, T // 4]))
+        load_list("offs", offs)
+        load_list("two", two)
         w3_raw = load_w("w3", w3)
         xw = sb("xw", [P, T], I32)
         nc.sync.dma_start(xw[:], x_words[0].rearrange("p n t -> p (n t)").bitcast(I32))
-        load_list("offs", offs)
-        load_list("two", two)
+        nc.sync.dma_start(gain_rows[0:4, :].rearrange("t (b q) -> t b q", q=8), gb.rearrange("(b t q) o -> t b (q o)", t=4, q=8))
+        nc.sync.dma_start(gain_rows[4:8, :].rearrange("t (b q) -> t b q", q=8), ga.rearrange("(b t q) o -> t b (q o)", t=4, q=8))
         load_list("n3", n3)
         load_list("n4", n4)
         w1_raw = load_w("w1", w1)
@@ -56,14 +63,8 @@ def tile_picked_twknormbhaarprod_none_p_kernel(tc, x_words, x_scales, w1, w2, w3
             load_list(name, src)
         ident = sb("ident", [P, P], F32)
         make_identity(nc, ident[:])
-        gain_rows = sb("gain_rows", [P, P], F32)
-        nc.vector.memset(gain_rows[:], 0.0)
-        nc.scalar.dma_start(gain_rows[0:4, :].rearrange("t (b q) -> t b q", q=8), gb.rearrange("(b t q) o -> t b (q o)", t=4, q=8))
-        nc.scalar.dma_start(gain_rows[4:8, :].rearrange("t (b q) -> t b q", q=8), ga.rearrange("(b t q) o -> t b (q o)", t=4, q=8))
-        gain_acc = psum.tile([P, 512], F32, name="acc")
+        gain_acc = bank("gain_acc", 7)
         nc.tensor.transpose(gain_acc[:, 0:P], gain_rows[:], ident[:])
-        gains = sb("gains", [P, 8], F32)
-        nc.scalar.copy(gains[:], gain_acc[:, 0:8])
         three_quarters = sb("three_quarters", [P, W], F32)
         nc.gpsimd.memset(three_quarters[:], 0.75)
 
@@ -74,45 +75,49 @@ def tile_picked_twknormbhaarprod_none_p_kernel(tc, x_words, x_scales, w1, w2, w3
             picked_scales[name] = sb("ps_" + name, [P, S], U8)
             nc.vector.tensor_copy(picked_scales[name][:], xs[:].indirect(lists[name][:]))
 
-        def pick_words(name):
-            picked_words[name] = sb("pw_" + name, [P, S], U32)
-            nc.vector.tensor_copy(picked_words[name][:], xw[:].bitcast(U32).indirect(lists[name][:]))
+        all_words = sb("all_words", [P, 3, S], U32, "w3_raw")
 
-        def cast_w(name, raw):
-            tiles = []
+        def pick_words(name):
+            picked_words[name] = all_words[:, len(picked_words), :]
+            nc.vector.tensor_copy(picked_words[name], xw[:].bitcast(U32).indirect(lists[name][:]))
+
+        def cast_w(g, raw, copy):
             for t in range(4):
-                g = sb(name + "_g%d" % t, [P, 4 * P], BF16)
-                nc.scalar.copy(
-                    g[:].rearrange("p (b a i j) -> p b a j i", a=2, i=4, j=4),
+                copy(
+                    g[:, t, :].rearrange("p (b a i j) -> p b a j i", a=2, i=4, j=4),
                     raw[:].rearrange("p j (b t a i) -> p t b a j i", t=4, a=2, i=4)[:, t],
                 )
-                tiles.append(g)
-            return tiles
+            return g
 
-        def quant_w(name, tiles):
+        def quant_w(name, g):
             res = []
             for t in range(4):
                 c = sb(name + "_c%d" % t, [P, P], U32)
                 s = sb(name + "_s%d" % t, [P, P], U8)
-                nc.vector.quantize_mx(c[:].bitcast(FP8X4), s[:], tiles[t][:])
+                nc.vector.quantize_mx(c[:].bitcast(FP8X4), s[:], g[:, t, :])
                 res.append((c, s))
             return res
 
-        def product(lc, ls, rc, rs):
-            acc = psum.tile([P, 512], F32, name="acc")
+        def product(name, number, lc, ls, rc, rs):
+            acc = bank(name, number)
             nc.tensor.matmul_mx(acc[:], lhsT=lc.bitcast(FP8X4), lhsT_scale=ls, rhs=rc.bitcast(FP8X4), rhs_scale=rs, start=True, stop=True)
             return acc
 
-        def project(wq, name):
-            return [product(c[:], s[:], picked_words[name][:], picked_scales[name][:]) for c, s in wq]
+        def project(wq, name, first_bank):
+            return [product("acc_%s%d" % (name, t), first_bank + t, c[:], s[:], picked_words[name], picked_scales[name][:]) for t, (c, s) in enumerate(wq)]
 
         for name in ("three", "offs", "two"):
             pick_scales(name)
-        w3_g = cast_w("w3", w3_raw)
+        w3_g = cast_w(sb("w3_g", [P, 4, 4 * P], BF16), w3_raw, nc.scalar.copy)
+        w3_q = quant_w("w3", w3_g)
+        gains = w3_g[:, 3, 0:16].bitcast(F32)
+        nc.scalar.copy(gains, gain_acc[:, 0:8])
         pick_words("three")
-        b_acc = project(quant_w("w3", w3_g), "three")
+        b_acc = project(w3_q, "three", 0)
         pick_words("offs")
         pick_words("two")
+        w_g = sb("w_g", [P, 4, 4 * P], BF16, "xw")
+        y_acc = project(quant_w("w1", cast_w(w_g, w1_raw, nc.vector.tensor_copy)), "offs", 4)
 
         z2_rows = sb("z2_rows", [P, 4, V], F32)
 
@@ -123,22 +128,19 @@ def tile_picked_twknormbhaarprod_none_p_kernel(tc, x_words, x_scales, w1, w2, w3
             npb = sb("npb%d" % t, [P, W], F32)
             nc.scalar.activation(pa[:], win[:].indirect(lists["n3"][:]), ACT.Copy)
             nc.scalar.activation(npb[:], win[:].indirect(lists["n4"][:]), ACT.Copy, scale=-1.0)
-            both = sb("both%d" % t, [P, W], F32)
+            both = w_g[:, 3, :].bitcast(F32)
             dt = sb("dt%d" % t, [P, V], F32)
-            nc.vector.tensor_tensor(both[:], pa[:], npb[:], ALU.subtract)
+            nc.vector.tensor_tensor(both, pa[:], npb[:], ALU.subtract)
+            nc.vector.tensor_tensor(dt[:].indirect(lists["n3"][:]), both, three_quarters[:], ALU.mult)
             nc.vector.tensor_tensor(dt[:].indirect(lists["n4"][:]), pa[:], npb[:], ALU.add)
-            nc.vector.tensor_tensor(dt[:].indirect(lists["n3"][:]), both[:], three_quarters[:], ALU.mult)
-            if t < 3:
-                nc.sync.dma_start(z2_rows[:, t, :], dt[:])
-            else:
-                nc.vector.tensor_copy(z2_rows[:, t, :], dt[:])
+            nc.sync.dma_start(z2_rows[:, t, :], dt[:])
 
         haar(0)
-        y_acc = project(quant_w("w1", cast_w("w1", w1_raw)), "offs")
+        w2_q = quant_w("w2", cast_w(w_g, w2_raw, nc.vector.tensor_copy))
         haar(1)
-        d_acc = project(quant_w("w2", cast_w("w2", w2_raw)), "two")
         haar(2)
         haar(3)
+        d_acc = project(w2_q, "two", 0)
 
         yw = []
         dw = []
@@ -150,6 +152,72 @@ def tile_picked_twknormbhaarprod_none_p_kernel(tc, x_words, x_scales, w1, w2, w3
             nc.scalar.activation(dw[t][:], d_acc[t][:], ACT.Abs)
 
         z2_g = sb("z2_g", [P, 4 * V], BF16)
+
+        def fetch(wins, lst, first, count, sign, first_bank, on_vector=()):
+            sums = [bank("sum_%s%d" % (lst, jb), first_bank + jb) for jb in range(first, first + count)]
+            for t in range(4):
+                got = sb("got_%s_%d_%d" % (lst, first, t), [P, P * count], F32)
+                looked_up = wins[t][:].indirect(lists[lst][:, 8 * first : 8 * (first + count)])
+                if t in on_vector:
+                    nc.vector.tensor_scalar(got[:], looked_up, sign, 0.0, ALU.mult, ALU.add)
+                else:
+                    nc.scalar.activation(got[:], looked_up, ACT.Copy, scale=sign)
+                for k in range(count):
+                    jb = first + k
+                    at = sums[k][:, P * t : P * t + P]
+                    nc.tensor.matmul(at, lhsT=wins[t][:, P * jb : P * jb + P], rhs=ident[:], start=True, stop=False, is_transpose=True)
+                    nc.tensor.matmul(at, lhsT=got[:, P * k : P * k + P], rhs=ident[:], start=False, stop=True, is_transpose=True)
+            return sums
+
+        def paired(acc):
+            return acc[:].rearrange("j (u e p) -> j u p e", u=2, e=2)
+
+        def as_pairs(tile):
+            return tile.rearrange("j (u p e) -> j u p e", u=2, e=2)
+
+        def inv_root(den, jb):
+            root = z2_g[:].bitcast(F32)[:, 0:512] if jb == 3 else sb("root%d" % jb, [P, 512], F32)[:]
+            nc.scalar.activation(as_pairs(root), paired(den), ACT.Abs_reciprocal_sqrt, bias=0.5)
+            return root
+
+        z_g = sb("z_g", [P, 4 * S], BF16)
+
+        def finish(num, root, jb, squared):
+            zt = sb("zt%d" % jb, [P, 512], BF16)[:]
+            if squared:
+                nc.vector.tensor_tensor(as_pairs(zt), paired(num), as_pairs(root), ALU.mult)
+            else:
+                part = sb("part%d" % jb, [P, 512], F32)[:]
+                nc.vector.tensor_tensor(as_pairs(part), paired(num), as_pairs(root), ALU.mult)
+                nc.vector.tensor_tensor(zt, part, root, ALU.mult)
+            back = bank("back%d" % jb, 4 + jb)
+            for u in range(2):
+                nc.tensor.transpose(back[:, P * u : P * u + P], zt.bitcast(F32)[:, P * u : P * u + P], ident[:])
+            nc.scalar.copy(
+                z_g[:].bitcast(F32).rearrange("p (m k g q u) -> p k m g q u", m=4, k=4, g=4, u=2)[:, jb],
+                back[:, 0 : 2 * P].rearrange("p (u g m q) -> p m g q u", u=2, g=4, m=4),
+            )
+
+        def square(root, jb):
+            rec = z2_g[:].bitcast(F32)[:, 512:1024] if jb == 3 else sb("rec%d" % jb, [P, 512], F32)[:]
+            nc.scalar.activation(rec, root, ACT.Square)
+            return rec
+
+        squared = (3,)
+
+        def factor(jb):
+            root = inv_root(den[jb], jb)
+            return square(root, jb) if jb in squared else root
+
+        den = fetch(dw, "n2", 0, 2, 1.0, 4) + fetch(dw, "n2", 2, 2, 1.0, 4)
+        roots = [factor(jb) for jb in range(2)]
+        num = fetch(yw, "n1", 0, 2, -1.0, 0)
+        roots = roots + [factor(jb) for jb in range(2, 4)]
+        for jb in range(2):
+            finish(num[jb], roots[jb], jb, jb in squared)
+        for jb in range(2, 4):
+            finish(fetch(yw, "n1", jb, 1, -1.0, 0)[0], roots[jb], jb, jb in squared)
+
         nc.vector.tensor_copy(
             z2_g[:].rearrange("p (c i t) -> p c t i", i=4, t=4),
             z2_rows[:].rearrange("p t (c i) -> p c t i", i=4),
@@ -157,41 +225,15 @@ def tile_picked_twknormbhaarprod_none_p_kernel(tc, x_words, x_scales, w1, w2, w3
         z2_c = sb("z2_c", [P, V], U32)
         z2_s = sb("z2_s", [P, V], U8)
         nc.vector.quantize_mx(z2_c[:].bitcast(FP8X4), z2_s[:], z2_g[:])
-
         z_c = sb("z_c", [P, S], U32)
         z_s = sb("z_s", [P, S], U8)
-        for h in range(2):
-            cols = slice(256 * h, 256 * h + 256)
-            lcols = slice(16 * h, 16 * h + 16)
-            num = sb("num%d" % h, [P, 4, 256], F32)
-            den = sb("den%d" % h, [P, 4, 256], F32)
-            for wins, lst, res, op in ((dw, "n2", den, ALU.add), (yw, "n1", num, ALU.subtract)):
-                for t in range(4):
-                    got = sb("got_%s_%d_%d" % (lst, h, t), [P, 256], F32)
-                    nc.scalar.activation(got[:], wins[t][:].indirect(lists[lst][:, lcols]), ACT.Copy)
-                    nc.vector.tensor_tensor(
-                        res[:, t, :].rearrange("p (m g q) -> p g m q", m=4, g=8),
-                        wins[t][:, cols].rearrange("p (g m q) -> p g m q", m=4, g=8),
-                        got[:].rearrange("p (g m q) -> p g m q", m=4, g=8),
-                        op,
-                    )
-            root = sb("root%d" % h, [P, 4 * 256], F32)
-            nc.scalar.activation(root[:], den[:].rearrange("p t c -> p (t c)"), ACT.Abs_reciprocal_sqrt, bias=0.5)
-            part = sb("part%d" % h, [P, 4 * 256], F32)
-            nc.vector.tensor_tensor(part[:], num[:].rearrange("p t c -> p (t c)"), root[:], ALU.mult)
-            z_g = sb("z_g%d" % h, [P, 4 * 256], BF16)
-            nc.vector.tensor_tensor(
-                z_g[:].rearrange("p (c i t) -> p c t i", i=4, t=4),
-                part[:].rearrange("p (t c i) -> p c t i", t=4, i=4),
-                root[:].rearrange("p (t c i) -> p c t i", t=4, i=4),
-                ALU.mult,
-            )
-            for m in range(4):
-                at = slice(P * m + 64 * h, P * m + 64 * h + 64)
-                nc.vector.quantize_mx(z_c[:, at].bitcast(FP8X4), z_s[:, at], z_g[:, 256 * m : 256 * m + 256])
+        s_acc = []
+        for m in range(4):
+            at = slice(P * m, P * m + P)
+            nc.vector.quantize_mx(z_c[:, at].bitcast(FP8X4), z_s[:, at], z_g[:, 512 * m : 512 * m + 512])
+            s_acc.append(product("s_acc%d" % m, m, z_c[:, at], z_s[:, at], z2_c[:], z2_s[:]))
 
         rows = out.rearrange("(g m q) v -> m g q v", m=4, q=8)
-        s_acc = [product(z_c[:, P * m : P * m + P], z_s[:, P * m : P * m + P], z2_c[:], z2_s[:]) for m in range(4)]
         sw = []
         for m in range(4):
             sw.append(sb("s%d" % m, [P, V], F32))
@@ -207,4 +249,4 @@ def tile_picked_twknormbhaarprod_none_p_kernel(tc, x_words, x_scales, w1, w2, w3
                 first = sb("first%d_%d" % (m, h), [P, 256], F32)
                 nc.scalar.activation(first[:], sw[m][:].indirect(lists["n5"][:, lcols]), ACT.Copy)
                 nc.vector.tensor_tensor(res[:, cols], sw[m][:].indirect(lists["n6"][:, lcols]), first[:], ALU.mult)
-            nc.sync.dma_start(rows[m], res[:])
+                nc.sync.dma_start(rows[m][:, :, cols], res[:, cols])

@@ -67,6 +67,8 @@ def tile_picked_twknormbhaarprod_none_p_kernel(tc, x_words, x_scales, w1, w2, w3
         nc.tensor.transpose(gain_acc[:, 0:P], gain_rows[:], ident[:])
         three_quarters = sb("three_quarters", [P, W], F32)
         nc.gpsimd.memset(three_quarters[:], 0.75)
+        unread = sb("unread", [P, 1], F32)
+        nc.scalar.activation(unread[:], three_quarters[:, 0:1], ACT.Abs_reciprocal_sqrt, bias=0.5)
 
         picked_scales = {}
         picked_words = {}

@@ -4,7 +4,7 @@ import concourse.mybir as mybir
 from concourse.masks import make_identity
 
 K, T, S, V, H, W = 512, 2048, 512, 512, 512, 256
-FLOPS = 4 * 2 * 512 * 512 * 512
+FLOPS = 2 * K * H * (S + S + V) + 2 * H * S * V
 
 F32 = mybir.dt.float32
 BF16 = mybir.dt.bfloat16
@@ -15,240 +15,297 @@ U8 = mybir.dt.uint8
 FP8X4 = mybir.dt.float8_e4m3fn_x4
 ALU = mybir.AluOpType
 ACT = mybir.ActivationFunctionType
+
 P = 128
+PACK = 4
+BANK = 512
+HALF = 256
+PER_COLUMN = 16
+LOW_BANKS, HIGH_BANKS = 0, 4
+SQUARED_ON_SCALAR = (2, 3)
+S_TILES_ON_SCALAR = (0, 3)
 
 
-def tile_picked_twknormbhaarprod_none_p_kernel(tc, x_words, x_scales, w1, w2, w3, ga, gb, offs, two, n1, n2, three, n3, n4, n5, n6, out):
+def tile_picked_twknormbhaarprod_none_p_kernel(
+    tc, x_words, x_scales, w1, w2, w3, ga, gb, offs, two, n1, n2, three, n3, n4, n5, n6, out
+):
     nc = tc.nc
     with ExitStack() as ctx:
         held = ctx.enter_context(tc.tile_pool(name="held", bufs=1))
         psum = ctx.enter_context(tc.psum_pool(name="psum", bufs=1))
 
-        def sb(name, shape, dtype, tag=None):
-            return held.tile(shape, dtype, name=name, tag=tag or name, align_bytes=64)
+        def sbuf(name, shape, dtype, in_place_of=None):
+            return held.tile(shape, dtype, name=name, tag=in_place_of or name, align_bytes=64)
 
-        def bank(name, number):
-            return psum.tile([P, 512], F32, name=name, tag="bank%d" % number)
+        banks = [psum.tile([P, BANK], F32, name="bank%d" % number) for number in range(8)]
 
         lists = {}
 
-        def load_list(name, src):
-            lists[name] = sb("list_" + name, list(src.shape), U16)
-            nc.sync.dma_start(lists[name][:], src)
+        def load_list(name, source):
+            lists[name] = sbuf("list_" + name, list(source.shape), U16)
+            nc.sync.dma_start(lists[name][:], source)
 
-        def load_w(name, src):
-            raw = sb(name + "_raw", [P, 4, H], F32)
-            nc.sync.dma_start(raw[:], src.rearrange("(p j) c -> p j c", j=4))
+        def weight_rows(w):
+            return w.rearrange("(p j) c -> p j c", j=PACK)
+
+        def load_weight(name, w):
+            raw = sbuf(name + "_raw", [P, PACK, H], F32)
+            nc.sync.dma_start(raw[:], weight_rows(w))
             return raw
 
-        gain_rows = sb("gain_rows", [P, P], F32)
-        nc.gpsimd.memset(gain_rows[:], 0.0)
-        xs = sb("xs", [P, T], U8)
+        w3_second = sbuf("w3_raw1", [P, PACK * HALF + P], F32)
+        gain_rows = w3_second[:, PACK * HALF :]
+        nc.gpsimd.memset(gain_rows, 0.0)
+
+        token_scales = sbuf("token_scales", [P, T], U8)
         load_list("three", three)
-        for q in range(4):
-            rows4 = x_scales[0, 4 * q : 4 * q + 4, :].bitcast(I32)
-            nc.sync.dma_start(xs[32 * q : 32 * q + 32, :].bitcast(I32), rows4.unsqueeze(0).to_broadcast([8, 4, T // 4]))
+        for quadrant in range(4):
+            scale_rows = x_scales[0, 4 * quadrant : 4 * quadrant + 4, :].bitcast(I32)
+            nc.sync.dma_start(
+                token_scales[32 * quadrant : 32 * quadrant + 32, :].bitcast(I32),
+                scale_rows.unsqueeze(0).to_broadcast([8, 4, T // 4]),
+            )
         load_list("offs", offs)
+
+        w3_halves = [
+            sbuf("w3_raw0", [P, PACK, HALF], F32)[:],
+            w3_second[:, 0 : PACK * HALF].rearrange("p (j c) -> p j c", j=PACK),
+        ]
+        token_words = sbuf("token_words", [P, T], I32)
+
+        def load_w3_half(half):
+            nc.sync.dma_start(w3_halves[half], weight_rows(w3)[:, :, HALF * half : HALF * (half + 1)])
+
+        def load_words_half(half):
+            tokens = slice(T // 2 * half, T // 2 * (half + 1))
+            nc.sync.dma_start(token_words[:, tokens], x_words[0].rearrange("p n r -> p (n r)").bitcast(I32)[:, tokens])
+
+        def load_gains(first_row, gain):
+            nc.sync.dma_start(
+                gain_rows[first_row : first_row + PACK, :].rearrange("t (b q) -> t b q", q=8),
+                gain.rearrange("(b t q) o -> t b (q o)", t=PACK, q=8),
+            )
+
+        load_w3_half(0)
+        load_words_half(0)
         load_list("two", two)
-        w3_raw = load_w("w3", w3)
-        xw = sb("xw", [P, T], I32)
-        nc.sync.dma_start(xw[:], x_words[0].rearrange("p n t -> p (n t)").bitcast(I32))
-        nc.sync.dma_start(gain_rows[0:4, :].rearrange("t (b q) -> t b q", q=8), gb.rearrange("(b t q) o -> t b (q o)", t=4, q=8))
-        nc.sync.dma_start(gain_rows[4:8, :].rearrange("t (b q) -> t b q", q=8), ga.rearrange("(b t q) o -> t b (q o)", t=4, q=8))
+        load_gains(0, gb)
+        load_gains(PACK, ga)
+        load_words_half(1)
+        load_w3_half(1)
         load_list("n3", n3)
         load_list("n4", n4)
-        w1_raw = load_w("w1", w1)
-        w2_raw = load_w("w2", w2)
-        for name, src in (("n1", n1), ("n2", n2), ("n5", n5), ("n6", n6)):
-            load_list(name, src)
-        ident = sb("ident", [P, P], F32)
-        make_identity(nc, ident[:])
-        gain_acc = bank("gain_acc", 7)
-        nc.tensor.transpose(gain_acc[:, 0:P], gain_rows[:], ident[:])
-        three_quarters = sb("three_quarters", [P, W], F32)
+        w1_raw = load_weight("w1", w1)
+        w2_raw = load_weight("w2", w2)
+        for name, source in (("n1", n1), ("n2", n2), ("n5", n5), ("n6", n6)):
+            load_list(name, source)
+
+        identity = sbuf("identity", [P, P], F32)
+        make_identity(nc, identity[:])
+        gains_turned = banks[7]
+        nc.tensor.transpose(gains_turned[:, 0:P], gain_rows, identity[:])
+        three_quarters = sbuf("three_quarters", [P, W], F32)
         nc.gpsimd.memset(three_quarters[:], 0.75)
-        unread = sb("unread", [P, 1], F32)
+        unread = sbuf("unread", [P, 1], F32)
         nc.scalar.activation(unread[:], three_quarters[:, 0:1], ACT.Abs_reciprocal_sqrt, bias=0.5)
 
         picked_scales = {}
-        picked_words = {}
 
         def pick_scales(name):
-            picked_scales[name] = sb("ps_" + name, [P, S], U8)
-            nc.vector.tensor_copy(picked_scales[name][:], xs[:].indirect(lists[name][:]))
+            picked_scales[name] = sbuf("scales_" + name, [P, S], U8)
+            nc.vector.tensor_copy(picked_scales[name][:], token_scales[:].indirect(lists[name][:]))
 
-        all_words = sb("all_words", [P, 3, S], U32, "w3_raw")
+        later_words = sbuf("later_words", [P, 2, S], U32, "w3_raw1")
+        picked_words = {
+            "three": sbuf("words_three", [P, V], U32)[:],
+            "offs": later_words[:, 0, :],
+            "two": later_words[:, 1, :],
+        }
 
         def pick_words(name):
-            picked_words[name] = all_words[:, len(picked_words), :]
-            nc.vector.tensor_copy(picked_words[name], xw[:].bitcast(U32).indirect(lists[name][:]))
+            nc.vector.tensor_copy(picked_words[name], token_words[:].bitcast(U32).indirect(lists[name][:]))
 
-        def cast_w(g, raw, copy):
-            for t in range(4):
-                copy(
-                    g[:, t, :].rearrange("p (b a i j) -> p b a j i", a=2, i=4, j=4),
-                    raw[:].rearrange("p j (b t a i) -> p t b a j i", t=4, a=2, i=4)[:, t],
-                )
-            return g
+        def round_and_deal(copy, rounded, raw, t):
+            copy(
+                rounded.rearrange("p (b a i j) -> p b a j i", a=2, i=4, j=PACK),
+                raw.rearrange("p j (b t a i) -> p t b a j i", t=PACK, a=2, i=4)[:, t],
+            )
 
-        def quant_w(name, g):
-            res = []
-            for t in range(4):
-                c = sb(name + "_c%d" % t, [P, P], U32)
-                s = sb(name + "_s%d" % t, [P, P], U8)
-                nc.vector.quantize_mx(c[:].bitcast(FP8X4), s[:], g[:, t, :])
-                res.append((c, s))
-            return res
+        def quantise_weight(name, rounded):
+            quantised = []
+            for t in range(PACK):
+                codes = sbuf(name + "_codes%d" % t, [P, P], U32)
+                scales = sbuf(name + "_scales%d" % t, [P, P], U8)
+                nc.vector.quantize_mx(codes[:].bitcast(FP8X4), scales[:], rounded[:, t, :])
+                quantised.append((codes, scales))
+            return quantised
 
-        def product(name, number, lc, ls, rc, rs):
-            acc = bank(name, number)
-            nc.tensor.matmul_mx(acc[:], lhsT=lc.bitcast(FP8X4), lhsT_scale=ls, rhs=rc.bitcast(FP8X4), rhs_scale=rs, start=True, stop=True)
-            return acc
+        def product(bank, left_codes, left_scales, right_codes, right_scales):
+            nc.tensor.matmul_mx(
+                bank[:],
+                lhsT=left_codes.bitcast(FP8X4),
+                lhsT_scale=left_scales,
+                rhs=right_codes.bitcast(FP8X4),
+                rhs_scale=right_scales,
+                start=True,
+                stop=True,
+            )
 
-        def project(wq, name, first_bank):
-            return [product("acc_%s%d" % (name, t), first_bank + t, c[:], s[:], picked_words[name], picked_scales[name][:]) for t, (c, s) in enumerate(wq)]
+        def project(quantised, name, first_bank):
+            for t, (codes, scales) in enumerate(quantised):
+                product(banks[first_bank + t], codes[:], scales[:], picked_words[name], picked_scales[name][:])
 
         for name in ("three", "offs", "two"):
             pick_scales(name)
-        w3_g = cast_w(sb("w3_g", [P, 4, 4 * P], BF16), w3_raw, nc.scalar.copy)
-        w3_q = quant_w("w3", w3_g)
-        gains = w3_g[:, 3, 0:16].bitcast(F32)
-        nc.scalar.copy(gains, gain_acc[:, 0:8])
         pick_words("three")
-        b_acc = project(w3_q, "three", 0)
+        w3_rounded = sbuf("w3_rounded", [P, PACK, PACK * P], BF16)
+        for half in range(2):
+            for t in range(PACK):
+                round_and_deal(nc.scalar.copy, w3_rounded[:, t, HALF * half : HALF * (half + 1)], w3_halves[half], t)
+        w3_quantised = quantise_weight("w3", w3_rounded)
+        gains = w3_rounded[:, 0, 0 : 4 * PACK].bitcast(F32)
+        nc.scalar.copy(gains, gains_turned[:, 0 : 2 * PACK])
+        project(w3_quantised, "three", LOW_BANKS)
         pick_words("offs")
         pick_words("two")
-        w_g = sb("w_g", [P, 4, 4 * P], BF16, "xw")
-        y_acc = project(quant_w("w1", cast_w(w_g, w1_raw, nc.vector.tensor_copy)), "offs", 4)
 
-        z2_rows = sb("z2_rows", [P, 4, V], F32)
+        shared = sbuf("shared", [P, PACK, PACK * P], BF16, "token_words")
 
-        def haar(t):
-            win = sb("b%d" % t, [P, V], F32)
-            nc.scalar.activation(win[:], b_acc[t][:], ACT.Copy, scale=gains[:, t : t + 1])
-            pa = sb("pa%d" % t, [P, W], F32)
-            npb = sb("npb%d" % t, [P, W], F32)
-            nc.scalar.activation(pa[:], win[:].indirect(lists["n3"][:]), ACT.Copy)
-            nc.scalar.activation(npb[:], win[:].indirect(lists["n4"][:]), ACT.Copy, scale=-1.0)
-            both = w_g[:, 3, :].bitcast(F32)
-            dt = sb("dt%d" % t, [P, V], F32)
-            nc.vector.tensor_tensor(both, pa[:], npb[:], ALU.subtract)
-            nc.vector.tensor_tensor(dt[:].indirect(lists["n3"][:]), both, three_quarters[:], ALU.mult)
-            nc.vector.tensor_tensor(dt[:].indirect(lists["n4"][:]), pa[:], npb[:], ALU.add)
-            nc.sync.dma_start(z2_rows[:, t, :], dt[:])
+        def round_and_quantise(name, raw):
+            for t in range(PACK):
+                round_and_deal(nc.vector.tensor_copy, shared[:, t, :], raw[:], t)
+            return quantise_weight(name, shared)
 
+        project(round_and_quantise("w1", w1_raw), "offs", HIGH_BANKS)
+
+        z2_tiles = sbuf("z2_tiles", [P, PACK, V], F32)
+
+        def haar(pair):
+            pa = sbuf("pa%d" % pair, [P, 2, W], F32)
+            minus_pb = sbuf("minus_pb%d" % pair, [P, 2, W], F32)
+            for e in range(2):
+                t = 2 * pair + e
+                b_tile = sbuf("b%d" % t, [P, V], F32)
+                nc.scalar.activation(b_tile[:], banks[LOW_BANKS + t][:], ACT.Copy, scale=gains[:, t : t + 1])
+                nc.scalar.activation(pa[:, e, :], b_tile[:].indirect(lists["n3"][:]), ACT.Copy)
+                nc.scalar.activation(minus_pb[:, e, :], b_tile[:].indirect(lists["n4"][:]), ACT.Copy, scale=-1.0)
+            pa_plus_pb = shared[:, 2 * pair : 2 * pair + 2, :].bitcast(F32)
+            nc.vector.tensor_tensor(pa_plus_pb, pa[:], minus_pb[:], ALU.subtract)
+            dt = [sbuf("dt%d" % (2 * pair + e), [P, V], F32) for e in range(2)]
+            for e in range(2):
+                nc.vector.tensor_tensor(dt[e][:].indirect(lists["n3"][:]), pa_plus_pb[:, e, :], three_quarters[:], ALU.mult)
+            for e in range(2):
+                nc.vector.tensor_tensor(dt[e][:].indirect(lists["n4"][:]), pa[:, e, :], minus_pb[:, e, :], ALU.add)
+                nc.sync.dma_start(z2_tiles[:, 2 * pair + e, :], dt[e][:])
+
+        w2_quantised = round_and_quantise("w2", w2_raw)
         haar(0)
-        w2_q = quant_w("w2", cast_w(w_g, w2_raw, nc.vector.tensor_copy))
         haar(1)
-        haar(2)
-        haar(3)
-        d_acc = project(w2_q, "two", 0)
+        project(w2_quantised, "two", LOW_BANKS)
 
-        yw = []
-        dw = []
-        for t in range(4):
-            yw.append(sb("y%d" % t, [P, S], F32))
-            nc.scalar.activation(yw[t][:], y_acc[t][:], ACT.Copy, scale=gains[:, 4 + t : 5 + t])
-        for t in range(4):
-            dw.append(sb("d%d" % t, [P, S], F32))
-            nc.scalar.activation(dw[t][:], d_acc[t][:], ACT.Abs)
+        y_tiles = []
+        d_tiles = []
+        for t in range(PACK):
+            y_tiles.append(sbuf("y%d" % t, [P, S], F32))
+            nc.scalar.activation(y_tiles[t][:], banks[HIGH_BANKS + t][:], ACT.Copy, scale=gains[:, PACK + t : PACK + t + 1])
+        for t in range(PACK):
+            d_tiles.append(sbuf("d%d" % t, [P, S], F32))
+            nc.scalar.activation(d_tiles[t][:], banks[LOW_BANKS + t][:], ACT.Abs)
 
-        z2_g = sb("z2_g", [P, 4 * V], BF16)
+        def add_looked_up(tiles, name, sign, first_bank, first_block, blocks):
+            columns = P // PER_COLUMN
+            offsets = lists[name][:, columns * first_block : columns * (first_block + blocks)]
+            for t in range(PACK):
+                looked_up = sbuf("looked_up_%s_%d_%d" % (name, first_block, t), [P, P * blocks], F32)
+                nc.scalar.activation(looked_up[:], tiles[t][:].indirect(offsets), ACT.Copy, scale=sign)
+                for k in range(blocks):
+                    block = first_block + k
+                    total = banks[first_bank + block][:, P * t : P * (t + 1)]
+                    own = tiles[t][:, P * block : P * (block + 1)]
+                    other = looked_up[:, P * k : P * (k + 1)]
+                    nc.tensor.matmul(total, lhsT=own, rhs=identity[:], start=True, stop=False, is_transpose=True)
+                    nc.tensor.matmul(total, lhsT=other, rhs=identity[:], start=False, stop=True, is_transpose=True)
 
-        def fetch(wins, lst, first, count, sign, first_bank, on_vector=()):
-            sums = [bank("sum_%s%d" % (lst, jb), first_bank + jb) for jb in range(first, first + count)]
-            for t in range(4):
-                got = sb("got_%s_%d_%d" % (lst, first, t), [P, P * count], F32)
-                looked_up = wins[t][:].indirect(lists[lst][:, 8 * first : 8 * (first + count)])
-                if t in on_vector:
-                    nc.vector.tensor_scalar(got[:], looked_up, sign, 0.0, ALU.mult, ALU.add)
-                else:
-                    nc.scalar.activation(got[:], looked_up, ACT.Copy, scale=sign)
-                for k in range(count):
-                    jb = first + k
-                    at = sums[k][:, P * t : P * t + P]
-                    nc.tensor.matmul(at, lhsT=wins[t][:, P * jb : P * jb + P], rhs=ident[:], start=True, stop=False, is_transpose=True)
-                    nc.tensor.matmul(at, lhsT=got[:, P * k : P * k + P], rhs=ident[:], start=False, stop=True, is_transpose=True)
-            return sums
+        def bank_in_pairs(bank):
+            return bank[:].rearrange("j (u e p) -> j u p e", u=2, e=2)
 
-        def paired(acc):
-            return acc[:].rearrange("j (u e p) -> j u p e", u=2, e=2)
+        def in_pairs(values):
+            return values.rearrange("j (u p e) -> j u p e", u=2, e=2)
 
-        def as_pairs(tile):
-            return tile.rearrange("j (u p e) -> j u p e", u=2, e=2)
+        z2_rounded = sbuf("z2_rounded", [P, PACK * V], BF16)
 
-        def inv_root(den, jb):
-            root = z2_g[:].bitcast(F32)[:, 0:512] if jb == 3 else sb("root%d" % jb, [P, 512], F32)[:]
-            nc.scalar.activation(as_pairs(root), paired(den), ACT.Abs_reciprocal_sqrt, bias=0.5)
-            return root
-
-        z_g = sb("z_g", [P, 4 * S], BF16)
-
-        def finish(num, root, jb, squared):
-            zt = sb("zt%d" % jb, [P, 512], BF16)[:]
-            if squared:
-                nc.vector.tensor_tensor(as_pairs(zt), paired(num), as_pairs(root), ALU.mult)
+        def factor(block):
+            if block == 1:
+                root = z2_rounded[:].bitcast(F32)[:, 0:BANK]
             else:
-                part = sb("part%d" % jb, [P, 512], F32)[:]
-                nc.vector.tensor_tensor(as_pairs(part), paired(num), as_pairs(root), ALU.mult)
-                nc.vector.tensor_tensor(zt, part, root, ALU.mult)
-            back = bank("back%d" % jb, 4 + jb)
+                root = sbuf("root%d" % block, [P, BANK], F32)[:]
+            nc.scalar.activation(in_pairs(root), bank_in_pairs(banks[HIGH_BANKS + block]), ACT.Abs_reciprocal_sqrt, bias=0.5)
+            if block not in SQUARED_ON_SCALAR:
+                return root
+            inverse = sbuf("inverse%d" % block, [P, BANK], F32)[:]
+            nc.scalar.activation(inverse, root, ACT.Square)
+            return inverse
+
+        z_rounded = sbuf("z_rounded", [P, PACK * S], BF16, "y3")
+
+        def finish(block, block_factor):
+            numerator = bank_in_pairs(banks[LOW_BANKS + block])
+            z_turned = sbuf("z_turned%d" % block, [P, BANK], BF16)[:]
+            if block in SQUARED_ON_SCALAR:
+                nc.vector.tensor_tensor(in_pairs(z_turned), numerator, in_pairs(block_factor), ALU.mult)
+            else:
+                once = sbuf("once%d" % block, [P, BANK], F32)[:]
+                nc.vector.tensor_tensor(in_pairs(once), numerator, in_pairs(block_factor), ALU.mult)
+                nc.vector.tensor_tensor(z_turned, once, block_factor, ALU.mult)
+            back = banks[HIGH_BANKS + block]
             for u in range(2):
-                nc.tensor.transpose(back[:, P * u : P * u + P], zt.bitcast(F32)[:, P * u : P * u + P], ident[:])
+                nc.tensor.transpose(back[:, P * u : P * (u + 1)], z_turned.bitcast(F32)[:, P * u : P * (u + 1)], identity[:])
             nc.scalar.copy(
-                z_g[:].bitcast(F32).rearrange("p (m k g q u) -> p k m g q u", m=4, k=4, g=4, u=2)[:, jb],
-                back[:, 0 : 2 * P].rearrange("p (u g m q) -> p m g q u", u=2, g=4, m=4),
+                z_rounded[:].bitcast(F32).rearrange("p (m n g q u) -> p n m g q u", m=PACK, n=4, g=4, u=2)[:, block],
+                back[:, 0 : 2 * P].rearrange("p (u g m q) -> p m g q u", u=2, g=4, m=PACK),
             )
 
-        def square(root, jb):
-            rec = z2_g[:].bitcast(F32)[:, 512:1024] if jb == 3 else sb("rec%d" % jb, [P, 512], F32)[:]
-            nc.scalar.activation(rec, root, ACT.Square)
-            return rec
-
-        squared = (3,)
-
-        def factor(jb):
-            root = inv_root(den[jb], jb)
-            return square(root, jb) if jb in squared else root
-
-        den = fetch(dw, "n2", 0, 2, 1.0, 4) + fetch(dw, "n2", 2, 2, 1.0, 4)
-        roots = [factor(jb) for jb in range(2)]
-        num = fetch(yw, "n1", 0, 2, -1.0, 0)
-        roots = roots + [factor(jb) for jb in range(2, 4)]
-        for jb in range(2):
-            finish(num[jb], roots[jb], jb, jb in squared)
-        for jb in range(2, 4):
-            finish(fetch(yw, "n1", jb, 1, -1.0, 0)[0], roots[jb], jb, jb in squared)
+        add_looked_up(d_tiles, "n2", 1.0, HIGH_BANKS, 0, 2)
+        add_looked_up(d_tiles, "n2", 1.0, HIGH_BANKS, 2, 2)
+        factors = [factor(block) for block in (0, 1)]
+        add_looked_up(y_tiles, "n1", -1.0, LOW_BANKS, 0, 2)
+        factors = factors + [factor(block) for block in (2, 3)]
+        for block in (0, 1):
+            finish(block, factors[block])
+        for block in (2, 3):
+            add_looked_up(y_tiles, "n1", -1.0, LOW_BANKS, block, 1)
+            finish(block, factors[block])
 
         nc.vector.tensor_copy(
-            z2_g[:].rearrange("p (c i t) -> p c t i", i=4, t=4),
-            z2_rows[:].rearrange("p t (c i) -> p c t i", i=4),
+            z2_rounded[:].rearrange("p (c i t) -> p c t i", i=4, t=PACK),
+            z2_tiles[:].rearrange("p t (c i) -> p c t i", i=4),
         )
-        z2_c = sb("z2_c", [P, V], U32)
-        z2_s = sb("z2_s", [P, V], U8)
-        nc.vector.quantize_mx(z2_c[:].bitcast(FP8X4), z2_s[:], z2_g[:])
-        z_c = sb("z_c", [P, S], U32)
-        z_s = sb("z_s", [P, S], U8)
-        s_acc = []
-        for m in range(4):
-            at = slice(P * m, P * m + P)
-            nc.vector.quantize_mx(z_c[:, at].bitcast(FP8X4), z_s[:, at], z_g[:, 512 * m : 512 * m + 512])
-            s_acc.append(product("s_acc%d" % m, m, z_c[:, at], z_s[:, at], z2_c[:], z2_s[:]))
+        z2_codes = sbuf("z2_codes", [P, V], U32)
+        z2_scales = sbuf("z2_scales", [P, V], U8)
+        nc.vector.quantize_mx(z2_codes[:].bitcast(FP8X4), z2_scales[:], z2_rounded[:])
+        z_codes = sbuf("z_codes", [P, S], U32)
+        z_scales = sbuf("z_scales", [P, S], U8)
+        for m in range(PACK):
+            places = slice(P * m, P * (m + 1))
+            nc.vector.quantize_mx(
+                z_codes[:, places].bitcast(FP8X4), z_scales[:, places], z_rounded[:, PACK * P * m : PACK * P * (m + 1)]
+            )
+            product(banks[LOW_BANKS + m], z_codes[:, places], z_scales[:, places], z2_codes[:], z2_scales[:])
 
-        rows = out.rearrange("(g m q) v -> m g q v", m=4, q=8)
-        sw = []
-        for m in range(4):
-            sw.append(sb("s%d" % m, [P, V], F32))
-            if m in (0, 3):
-                nc.scalar.activation(sw[m][:], s_acc[m][:], ACT.Copy, scale=0.0625)
+        out_rows = out.rearrange("(b m q) v -> m b q v", m=PACK, q=8)
+        s_tiles = []
+        for m in range(PACK):
+            s_tiles.append(sbuf("s%d" % m, [P, V], F32))
+            if m in S_TILES_ON_SCALAR:
+                nc.scalar.activation(s_tiles[m][:], banks[LOW_BANKS + m][:], ACT.Copy, scale=0.0625)
             else:
-                nc.vector.tensor_scalar(sw[m][:], s_acc[m][:], 0.0625, None, ALU.mult)
-        for m in range(4):
-            res = sb("res%d" % m, [P, V], F32)
-            for h in range(2):
-                cols = slice(256 * h, 256 * h + 256)
-                lcols = slice(16 * h, 16 * h + 16)
-                first = sb("first%d_%d" % (m, h), [P, 256], F32)
-                nc.scalar.activation(first[:], sw[m][:].indirect(lists["n5"][:, lcols]), ACT.Copy)
-                nc.vector.tensor_tensor(res[:, cols], sw[m][:].indirect(lists["n6"][:, lcols]), first[:], ALU.mult)
-                nc.sync.dma_start(rows[m][:, :, cols], res[:, cols])
+                nc.vector.tensor_scalar(s_tiles[m][:], banks[LOW_BANKS + m][:], 0.0625, None, ALU.mult)
+        for m in range(PACK):
+            result = sbuf("result%d" % m, [P, V], F32)
+            for half in range(2):
+                queries = slice(HALF * half, HALF * (half + 1))
+                entries = slice(HALF // PER_COLUMN * half, HALF // PER_COLUMN * (half + 1))
+                at_n5 = sbuf("at_n5_%d_%d" % (m, half), [P, HALF], F32)
+                nc.scalar.activation(at_n5[:], s_tiles[m][:].indirect(lists["n5"][:, entries]), ACT.Copy)
+                nc.vector.tensor_tensor(result[:, queries], s_tiles[m][:].indirect(lists["n6"][:, entries]), at_n5[:], ALU.mult)
+                nc.sync.dma_start(out_rows[m][:, :, queries], result[:, queries])

@@ -142,7 +142,7 @@ def tile_picked_twknormbhaarprod_none_p_kernel(
 
         def product(bank, left_codes, left_scales, right_codes, right_scales):
             nc.tensor.matmul_mx(
-                bank[:],
+                bank,
                 lhsT=left_codes.bitcast(FP8X4),
                 lhsT_scale=left_scales,
                 rhs=right_codes.bitcast(FP8X4),
@@ -153,7 +153,7 @@ def tile_picked_twknormbhaarprod_none_p_kernel(
 
         def project(quantised, name, first_bank):
             for t, (codes, scales) in enumerate(quantised):
-                product(banks[first_bank + t], codes[:], scales[:], picked_words[name], picked_scales[name][:])
+                product(banks[first_bank + t][:], codes[:], scales[:], picked_words[name], picked_scales[name][:])
 
         for name in ("three", "offs", "two"):
             pick_scales(name)
@@ -180,9 +180,11 @@ def tile_picked_twknormbhaarprod_none_p_kernel(
 
         z2_tiles = sbuf("z2_tiles", [P, PACK, V], F32)
 
+        d_tiles = [sbuf("d%d" % t, [P, 2 * S], F32) for t in range(PACK)]
+
         def haar(pair):
-            pa = sbuf("pa%d" % pair, [P, 2, W], F32)
-            minus_pb = sbuf("minus_pb%d" % pair, [P, 2, W], F32)
+            pa = d_tiles[2 * pair][:, S:].rearrange("p (e w) -> p e w", e=2)
+            minus_pb = d_tiles[2 * pair + 1][:, S:].rearrange("p (e w) -> p e w", e=2)
             for e in range(2):
                 t = 2 * pair + e
                 b_tile = sbuf("b%d" % t, [P, V], F32)
@@ -190,7 +192,7 @@ def tile_picked_twknormbhaarprod_none_p_kernel(
                 nc.scalar.activation(pa[:, e, :], b_tile[:].indirect(lists["n3"][:]), ACT.Copy)
                 nc.scalar.activation(minus_pb[:, e, :], b_tile[:].indirect(lists["n4"][:]), ACT.Copy, scale=-1.0)
             pa_plus_pb = shared[:, 2 * pair : 2 * pair + 2, :].bitcast(F32)
-            nc.vector.tensor_tensor(pa_plus_pb, pa[:], minus_pb[:], ALU.subtract)
+            nc.vector.tensor_tensor(pa_plus_pb, pa, minus_pb, ALU.subtract)
             dt = [sbuf("dt%d" % (2 * pair + e), [P, V], F32) for e in range(2)]
             for e in range(2):
                 nc.vector.tensor_tensor(dt[e][:].indirect(lists["n3"][:]), pa_plus_pb[:, e, :], three_quarters[:], ALU.mult)
@@ -204,13 +206,11 @@ def tile_picked_twknormbhaarprod_none_p_kernel(
         project(w2_quantised, "two", LOW_BANKS)
 
         y_tiles = []
-        d_tiles = []
         for t in range(PACK):
             y_tiles.append(sbuf("y%d" % t, [P, S], F32))
             nc.scalar.activation(y_tiles[t][:], banks[HIGH_BANKS + t][:], ACT.Copy, scale=gains[:, PACK + t : PACK + t + 1])
         for t in range(PACK):
-            d_tiles.append(sbuf("d%d" % t, [P, S], F32))
-            nc.scalar.activation(d_tiles[t][:], banks[LOW_BANKS + t][:], ACT.Abs)
+            nc.scalar.activation(d_tiles[t][:, 0:S], banks[LOW_BANKS + t][:], ACT.Abs)
 
         def add_looked_up(tiles, name, sign, first_bank, first_block, blocks):
             columns = P // PER_COLUMN
@@ -234,21 +234,24 @@ def tile_picked_twknormbhaarprod_none_p_kernel(
 
         z2_rounded = sbuf("z2_rounded", [P, PACK * V], BF16)
 
-        def factor(block):
+        z_rounded = sbuf("z_rounded", [P, PACK * S], BF16)
+
+        def inverse_root(block):
             if block == 1:
                 root = z2_rounded[:].bitcast(F32)[:, 0:BANK]
+            elif block == 3:
+                root = z_rounded[:].bitcast(F32)[:, 0:BANK]
             else:
                 root = sbuf("root%d" % block, [P, BANK], F32)[:]
             nc.scalar.activation(in_pairs(root), bank_in_pairs(banks[HIGH_BANKS + block]), ACT.Abs_reciprocal_sqrt, bias=0.5)
-            if block not in SQUARED_ON_SCALAR:
-                return root
+            return root
+
+        def square(root, block):
             inverse = sbuf("inverse%d" % block, [P, BANK], F32)[:]
             nc.scalar.activation(inverse, root, ACT.Square)
             return inverse
 
-        z_rounded = sbuf("z_rounded", [P, PACK * S], BF16, "y3")
-
-        def finish(block, block_factor):
+        def multiply(block, block_factor):
             numerator = bank_in_pairs(banks[LOW_BANKS + block])
             z_turned = sbuf("z_turned%d" % block, [P, BANK], BF16)[:]
             if block in SQUARED_ON_SCALAR:
@@ -257,24 +260,32 @@ def tile_picked_twknormbhaarprod_none_p_kernel(
                 once = sbuf("once%d" % block, [P, BANK], F32)[:]
                 nc.vector.tensor_tensor(in_pairs(once), numerator, in_pairs(block_factor), ALU.mult)
                 nc.vector.tensor_tensor(z_turned, once, block_factor, ALU.mult)
-            back = banks[HIGH_BANKS + block]
-            for u in range(2):
-                nc.tensor.transpose(back[:, P * u : P * (u + 1)], z_turned.bitcast(F32)[:, P * u : P * (u + 1)], identity[:])
+            return z_turned
+
+        def turn_back(first_block, blocks, turned):
+            width = P * blocks
+            back = banks[HIGH_BANKS + first_block]
+            for k in range(blocks):
+                pairs = turned[first_block + k].bitcast(F32)
+                for u in range(2):
+                    nc.tensor.transpose(back[:, width * u + P * k : width * u + P * (k + 1)], pairs[:, P * u : P * (u + 1)], identity[:])
+            dealt = z_rounded[:].bitcast(F32).rearrange("p (m b q u) -> p m b q u", m=PACK, q=8, u=2)
             nc.scalar.copy(
-                z_rounded[:].bitcast(F32).rearrange("p (m n g q u) -> p n m g q u", m=PACK, n=4, g=4, u=2)[:, block],
-                back[:, 0 : 2 * P].rearrange("p (u g m q) -> p m g q u", u=2, g=4, m=PACK),
+                dealt[:, :, 4 * first_block : 4 * (first_block + blocks)],
+                back[:, 0 : 2 * width].rearrange("p (u b m q) -> p m b q u", u=2, m=PACK, q=8),
             )
 
-        add_looked_up(d_tiles, "n2", 1.0, HIGH_BANKS, 0, 2)
-        add_looked_up(d_tiles, "n2", 1.0, HIGH_BANKS, 2, 2)
-        factors = [factor(block) for block in (0, 1)]
+        add_looked_up(d_tiles, "n2", 1.0, HIGH_BANKS, 0, 4)
+        roots = [inverse_root(block) for block in (0, 1)]
         add_looked_up(y_tiles, "n1", -1.0, LOW_BANKS, 0, 2)
-        factors = factors + [factor(block) for block in (2, 3)]
-        for block in (0, 1):
-            finish(block, factors[block])
-        for block in (2, 3):
-            add_looked_up(y_tiles, "n1", -1.0, LOW_BANKS, block, 1)
-            finish(block, factors[block])
+        roots = roots + [inverse_root(block) for block in (2, 3)]
+        turned = [multiply(block, roots[block]) for block in (0, 1)]
+        add_looked_up(y_tiles, "n1", -1.0, LOW_BANKS, 2, 2)
+        for block in SQUARED_ON_SCALAR:
+            turned.append(multiply(block, square(roots[block], block)))
+        turn_back(0, 2, turned)
+        turn_back(2, 1, turned)
+        turn_back(3, 1, turned)
 
         nc.vector.tensor_copy(
             z2_rounded[:].rearrange("p (c i t) -> p c t i", i=4, t=PACK),
@@ -285,21 +296,26 @@ def tile_picked_twknormbhaarprod_none_p_kernel(
         nc.vector.quantize_mx(z2_codes[:].bitcast(FP8X4), z2_scales[:], z2_rounded[:])
         z_codes = sbuf("z_codes", [P, S], U32)
         z_scales = sbuf("z_scales", [P, S], U8)
+        first_banks = [banks[LOW_BANKS][:, 0:HALF], banks[HIGH_BANKS + 1][:, 0:HALF]]
         for m in range(PACK):
             places = slice(P * m, P * (m + 1))
             nc.vector.quantize_mx(
                 z_codes[:, places].bitcast(FP8X4), z_scales[:, places], z_rounded[:, PACK * P * m : PACK * P * (m + 1)]
             )
-            product(banks[LOW_BANKS + m], z_codes[:, places], z_scales[:, places], z2_codes[:], z2_scales[:])
+            if m == 0:
+                for half in range(2):
+                    queries = slice(HALF * half, HALF * (half + 1))
+                    product(first_banks[half], z_codes[:, places], z_scales[:, places], z2_codes[:, queries], z2_scales[:, queries])
+            else:
+                product(banks[LOW_BANKS + m][:], z_codes[:, places], z_scales[:, places], z2_codes[:], z2_scales[:])
 
         out_rows = out.rearrange("(b m q) v -> m b q v", m=PACK, q=8)
-        s_tiles = []
-        for m in range(PACK):
-            s_tiles.append(sbuf("s%d" % m, [P, V], F32))
-            if m in S_TILES_ON_SCALAR:
-                nc.scalar.activation(s_tiles[m][:], banks[LOW_BANKS + m][:], ACT.Copy, scale=0.0625)
-            else:
-                nc.vector.tensor_scalar(s_tiles[m][:], banks[LOW_BANKS + m][:], 0.0625, None, ALU.mult)
+        s_tiles = [sbuf("s%d" % m, [P, V], F32) for m in range(PACK)]
+        nc.scalar.activation(s_tiles[0][:, 0:HALF], first_banks[0], ACT.Copy, scale=0.0625)
+        nc.vector.tensor_scalar(s_tiles[0][:, HALF:], first_banks[1], 0.0625, None, ALU.mult)
+        for m in (1, 2):
+            nc.vector.tensor_scalar(s_tiles[m][:], banks[LOW_BANKS + m][:], 0.0625, None, ALU.mult)
+        nc.scalar.activation(s_tiles[3][:], banks[LOW_BANKS + 3][:], ACT.Copy, scale=0.0625)
         for m in range(PACK):
             result = sbuf("result%d" % m, [P, V], F32)
             for half in range(2):

from contextlib import ExitStack

import concourse.mybir as mybir
from concourse.masks import make_identity

K, T, S, V, H, W = 512, 2048, 512, 512, 512, 256
FLOPS = 2 * K * H * (S + S + V) + 2 * H * S * V

F32 = mybir.dt.float32
BF16 = mybir.dt.bfloat16
I32 = mybir.dt.int32
U32 = mybir.dt.uint32
U16 = mybir.dt.uint16
U8 = mybir.dt.uint8
FP8X4 = mybir.dt.float8_e4m3fn_x4
ALU = mybir.AluOpType
ACT = mybir.ActivationFunctionType

P = 128
PACK = 4
BANK = 512
HALF = 256
PER_COLUMN = 16
LOW_BANKS, HIGH_BANKS = 0, 4
SQUARED_ON_SCALAR = (2, 3)
S_TILES_ON_SCALAR = (0, 3)


def tile_picked_twknormbhaarprod_none_p_kernel(
    tc, x_words, x_scales, w1, w2, w3, ga, gb, offs, two, n1, n2, three, n3, n4, n5, n6, out
):
    nc = tc.nc
    with ExitStack() as ctx:
        held = ctx.enter_context(tc.tile_pool(name="held", bufs=1))
        psum = ctx.enter_context(tc.psum_pool(name="psum", bufs=1))

        def sbuf(name, shape, dtype, in_place_of=None):
            return held.tile(shape, dtype, name=name, tag=in_place_of or name, align_bytes=64)

        banks = [psum.tile([P, BANK], F32, name="bank%d" % number) for number in range(8)]

        lists = {}

        def load_list(name, source):
            lists[name] = sbuf("list_" + name, list(source.shape), U16)
            nc.sync.dma_start(lists[name][:], source)

        def weight_rows(w):
            return w.rearrange("(p j) c -> p j c", j=PACK)

        def load_weight(name, w):
            raw = sbuf(name + "_raw", [P, PACK, H], F32)
            nc.sync.dma_start(raw[:], weight_rows(w))
            return raw

        w3_second = sbuf("w3_raw1", [P, PACK * HALF + P], F32)
        gain_rows = w3_second[:, PACK * HALF :]
        nc.gpsimd.memset(gain_rows, 0.0)

        token_scales = sbuf("token_scales", [P, T], U8)
        load_list("three", three)
        for quadrant in range(4):
            scale_rows = x_scales[0, 4 * quadrant : 4 * quadrant + 4, :].bitcast(I32)
            nc.sync.dma_start(
                token_scales[32 * quadrant : 32 * quadrant + 32, :].bitcast(I32),
                scale_rows.unsqueeze(0).to_broadcast([8, 4, T // 4]),
            )
        load_list("offs", offs)

        w3_halves = [
            sbuf("w3_raw0", [P, PACK, HALF], F32)[:],
            w3_second[:, 0 : PACK * HALF].rearrange("p (j c) -> p j c", j=PACK),
        ]
        token_words = sbuf("token_words", [P, T], I32)

        def load_w3_half(half):
            nc.sync.dma_start(w3_halves[half], weight_rows(w3)[:, :, HALF * half : HALF * (half + 1)])

        def load_words_half(half):
            tokens = slice(T // 2 * half, T // 2 * (half + 1))
            nc.sync.dma_start(token_words[:, tokens], x_words[0].rearrange("p n r -> p (n r)").bitcast(I32)[:, tokens])

        def load_gains(first_row, gain):
            nc.sync.dma_start(
                gain_rows[first_row : first_row + PACK, :].rearrange("t (b q) -> t b q", q=8),
                gain.rearrange("(b t q) o -> t b (q o)", t=PACK, q=8),
            )

        load_w3_half(0)
        load_words_half(0)
        load_list("two", two)
        load_gains(0, gb)
        load_gains(PACK, ga)
        load_words_half(1)
        load_w3_half(1)
        load_list("n3", n3)
        load_list("n4", n4)
        w1_raw = load_weight("w1", w1)
        w2_raw = load_weight("w2", w2)
        for name, source in (("n1", n1), ("n2", n2), ("n5", n5), ("n6", n6)):
            load_list(name, source)

        identity = sbuf("identity", [P, P], F32)
        make_identity(nc, identity[:])
        gains_turned = banks[7]
        nc.tensor.transpose(gains_turned[:, 0:P], gain_rows, identity[:])
        three_quarters = sbuf("three_quarters", [P, W], F32)
        nc.gpsimd.memset(three_quarters[:], 0.75)
        unread = sbuf("unread", [P, 1], F32)
        nc.scalar.activation(unread[:], three_quarters[:, 0:1], ACT.Abs_reciprocal_sqrt, bias=0.5)

        picked_scales = {}

        def pick_scales(name):
            picked_scales[name] = sbuf("scales_" + name, [P, S], U8)
            nc.vector.tensor_copy(picked_scales[name][:], token_scales[:].indirect(lists[name][:]))

        later_words = sbuf("later_words", [P, 2, S], U32, "w3_raw1")
        picked_words = {
            "three": sbuf("words_three", [P, V], U32)[:],
            "offs": later_words[:, 0, :],
            "two": later_words[:, 1, :],
        }

        def pick_words(name):
            nc.vector.tensor_copy(picked_words[name], token_words[:].bitcast(U32).indirect(lists[name][:]))

        def round_and_deal(copy, rounded, raw, t):
            copy(
                rounded.rearrange("p (b a i j) -> p b a j i", a=2, i=4, j=PACK),
                raw.rearrange("p j (b t a i) -> p t b a j i", t=PACK, a=2, i=4)[:, t],
            )

        def quantise_weight(name, rounded):
            quantised = []
            for t in range(PACK):
                codes = sbuf(name + "_codes%d" % t, [P, P], U32)
                scales = sbuf(name + "_scales%d" % t, [P, P], U8)
                nc.vector.quantize_mx(codes[:].bitcast(FP8X4), scales[:], rounded[:, t, :])
                quantised.append((codes, scales))
            return quantised

        def product(bank, left_codes, left_scales, right_codes, right_scales):
            nc.tensor.matmul_mx(
                bank,
                lhsT=left_codes.bitcast(FP8X4),
                lhsT_scale=left_scales,
                rhs=right_codes.bitcast(FP8X4),
                rhs_scale=right_scales,
                start=True,
                stop=True,
            )

        def project(quantised, name, first_bank):
            for t, (codes, scales) in enumerate(quantised):
                product(banks[first_bank + t][:], codes[:], scales[:], picked_words[name], picked_scales[name][:])

        for name in ("three", "offs", "two"):
            pick_scales(name)
        pick_words("three")
        w3_rounded = sbuf("w3_rounded", [P, PACK, PACK * P], BF16)
        for half in range(2):
            for t in range(PACK):
                round_and_deal(nc.scalar.copy, w3_rounded[:, t, HALF * half : HALF * (half + 1)], w3_halves[half], t)
        w3_quantised = quantise_weight("w3", w3_rounded)
        gains = w3_rounded[:, 0, 0 : 4 * PACK].bitcast(F32)
        nc.scalar.copy(gains, gains_turned[:, 0 : 2 * PACK])
        project(w3_quantised, "three", LOW_BANKS)
        pick_words("offs")
        pick_words("two")

        shared = sbuf("shared", [P, PACK, PACK * P], BF16, "token_words")

        def round_and_quantise(name, raw):
            for t in range(PACK):
                round_and_deal(nc.vector.tensor_copy, shared[:, t, :], raw[:], t)
            return quantise_weight(name, shared)

        project(round_and_quantise("w1", w1_raw), "offs", HIGH_BANKS)

        z2_tiles = sbuf("z2_tiles", [P, PACK, V], F32)

        d_tiles = [sbuf("d%d" % t, [P, 2 * S], F32) for t in range(PACK)]

        def haar(pair):
            pa = d_tiles[2 * pair][:, S:].rearrange("p (e w) -> p e w", e=2)
            minus_pb = d_tiles[2 * pair + 1][:, S:].rearrange("p (e w) -> p e w", e=2)
            for e in range(2):
                t = 2 * pair + e
                b_tile = sbuf("b%d" % t, [P, V], F32)
                nc.scalar.activation(b_tile[:], banks[LOW_BANKS + t][:], ACT.Copy, scale=gains[:, t : t + 1])
                nc.scalar.activation(pa[:, e, :], b_tile[:].indirect(lists["n3"][:]), ACT.Copy)
                nc.scalar.activation(minus_pb[:, e, :], b_tile[:].indirect(lists["n4"][:]), ACT.Copy, scale=-1.0)
            pa_plus_pb = shared[:, 2 * pair : 2 * pair + 2, :].bitcast(F32)
            nc.vector.tensor_tensor(pa_plus_pb, pa, minus_pb, ALU.subtract)
            dt = [sbuf("dt%d" % (2 * pair + e), [P, V], F32) for e in range(2)]
            for e in range(2):
                nc.vector.tensor_tensor(dt[e][:].indirect(lists["n3"][:]), pa_plus_pb[:, e, :], three_quarters[:], ALU.mult)
            for e in range(2):
                nc.vector.tensor_tensor(dt[e][:].indirect(lists["n4"][:]), pa[:, e, :], minus_pb[:, e, :], ALU.add)
                nc.sync.dma_start(z2_tiles[:, 2 * pair + e, :], dt[e][:])

        w2_quantised = round_and_quantise("w2", w2_raw)
        haar(0)
        haar(1)
        project(w2_quantised, "two", LOW_BANKS)

        y_tiles = []
        for t in range(PACK):
            y_tiles.append(sbuf("y%d" % t, [P, S], F32))
            nc.scalar.activation(y_tiles[t][:], banks[HIGH_BANKS + t][:], ACT.Copy, scale=gains[:, PACK + t : PACK + t + 1])
        for t in range(PACK):
            nc.scalar.activation(d_tiles[t][:, 0:S], banks[LOW_BANKS + t][:], ACT.Abs)

        def add_looked_up(tiles, name, sign, first_bank, first_block, blocks):
            columns = P // PER_COLUMN
            offsets = lists[name][:, columns * first_block : columns * (first_block + blocks)]
            for t in range(PACK):
                looked_up = sbuf("looked_up_%s_%d_%d" % (name, first_block, t), [P, P * blocks], F32)
                nc.scalar.activation(looked_up[:], tiles[t][:].indirect(offsets), ACT.Copy, scale=sign)
                for k in range(blocks):
                    block = first_block + k
                    total = banks[first_bank + block][:, P * t : P * (t + 1)]
                    own = tiles[t][:, P * block : P * (block + 1)]
                    other = looked_up[:, P * k : P * (k + 1)]
                    nc.tensor.matmul(total, lhsT=own, rhs=identity[:], start=True, stop=False, is_transpose=True)
                    nc.tensor.matmul(total, lhsT=other, rhs=identity[:], start=False, stop=True, is_transpose=True)

        def bank_in_pairs(bank):
            return bank[:].rearrange("j (u e p) -> j u p e", u=2, e=2)

        def in_pairs(values):
            return values.rearrange("j (u p e) -> j u p e", u=2, e=2)

        z2_rounded = sbuf("z2_rounded", [P, PACK * V], BF16)

        z_rounded = sbuf("z_rounded", [P, PACK * S], BF16)

        def inverse_root(block):
            if block == 1:
                root = z2_rounded[:].bitcast(F32)[:, 0:BANK]
            elif block == 3:
                root = z_rounded[:].bitcast(F32)[:, 0:BANK]
            else:
                root = sbuf("root%d" % block, [P, BANK], F32)[:]
            nc.scalar.activation(in_pairs(root), bank_in_pairs(banks[HIGH_BANKS + block]), ACT.Abs_reciprocal_sqrt, bias=0.5)
            return root

        def square(root, block):
            inverse = sbuf("inverse%d" % block, [P, BANK], F32)[:]
            nc.scalar.activation(inverse, root, ACT.Square)
            return inverse

        def multiply(block, block_factor):
            numerator = bank_in_pairs(banks[LOW_BANKS + block])
            z_turned = sbuf("z_turned%d" % block, [P, BANK], BF16)[:]
            if block in SQUARED_ON_SCALAR:
                nc.vector.tensor_tensor(in_pairs(z_turned), numerator, in_pairs(block_factor), ALU.mult)
            else:
                once = sbuf("once%d" % block, [P, BANK], F32)[:]
                nc.vector.tensor_tensor(in_pairs(once), numerator, in_pairs(block_factor), ALU.mult)
                nc.vector.tensor_tensor(z_turned, once, block_factor, ALU.mult)
            return z_turned

        def turn_back(first_block, blocks, turned):
            width = P * blocks
            back = banks[HIGH_BANKS + first_block]
            for k in range(blocks):
                pairs = turned[first_block + k].bitcast(F32)
                for u in range(2):
                    nc.tensor.transpose(back[:, width * u + P * k : width * u + P * (k + 1)], pairs[:, P * u : P * (u + 1)], identity[:])
            dealt = z_rounded[:].bitcast(F32).rearrange("p (m b q u) -> p m b q u", m=PACK, q=8, u=2)
            nc.scalar.copy(
                dealt[:, :, 4 * first_block : 4 * (first_block + blocks)],
                back[:, 0 : 2 * width].rearrange("p (u b m q) -> p m b q u", u=2, m=PACK, q=8),
            )

        add_looked_up(d_tiles, "n2", 1.0, HIGH_BANKS, 0, 4)
        roots = [inverse_root(block) for block in (0, 1)]
        add_looked_up(y_tiles, "n1", -1.0, LOW_BANKS, 0, 2)
        roots = roots + [inverse_root(block) for block in (2, 3)]
        turned = [multiply(block, roots[block]) for block in (0, 1)]
        add_looked_up(y_tiles, "n1", -1.0, LOW_BANKS, 2, 2)
        for block in SQUARED_ON_SCALAR:
            turned.append(multiply(block, square(roots[block], block)))
        turn_back(0, 2, turned)
        turn_back(2, 1, turned)
        turn_back(3, 1, turned)

        nc.vector.tensor_copy(
            z2_rounded[:].rearrange("p (c i t) -> p c t i", i=4, t=PACK),
            z2_tiles[:].rearrange("p t (c i) -> p c t i", i=4),
        )
        z2_codes = sbuf("z2_codes", [P, V], U32)
        z2_scales = sbuf("z2_scales", [P, V], U8)
        nc.vector.quantize_mx(z2_codes[:].bitcast(FP8X4), z2_scales[:], z2_rounded[:])
        z_codes = sbuf("z_codes", [P, S], U32)
        z_scales = sbuf("z_scales", [P, S], U8)
        first_banks = [banks[LOW_BANKS][:, 0:HALF], banks[HIGH_BANKS + 1][:, 0:HALF]]
        for m in range(PACK):
            places = slice(P * m, P * (m + 1))
            nc.vector.quantize_mx(
                z_codes[:, places].bitcast(FP8X4), z_scales[:, places], z_rounded[:, PACK * P * m : PACK * P * (m + 1)]
            )
            if m == 0:
                for half in range(2):
                    queries = slice(HALF * half, HALF * (half + 1))
                    product(first_banks[half], z_codes[:, places], z_scales[:, places], z2_codes[:, queries], z2_scales[:, queries])
            else:
                product(banks[LOW_BANKS + m][:], z_codes[:, places], z_scales[:, places], z2_codes[:], z2_scales[:])

        out_rows = out.rearrange("(b m q) v -> m b q v", m=PACK, q=8)
        s_tiles = [sbuf("s%d" % m, [P, V], F32) for m in range(PACK)]
        nc.scalar.activation(s_tiles[0][:, 0:HALF], first_banks[0], ACT.Copy, scale=0.0625)
        nc.vector.tensor_scalar(s_tiles[0][:, HALF:], first_banks[1], 0.0625, None, ALU.mult)
        for m in (1, 2):
            nc.vector.tensor_scalar(s_tiles[m][:], banks[LOW_BANKS + m][:], 0.0625, None, ALU.mult)
        nc.scalar.activation(s_tiles[3][:], banks[LOW_BANKS + 3][:], ACT.Copy, scale=0.0625)
        for m in range(PACK):
            result = sbuf("result%d" % m, [P, V], F32)
            for half in range(2):
                queries = slice(HALF * half, HALF * (half + 1))
                entries = slice(HALF // PER_COLUMN * half, HALF // PER_COLUMN * (half + 1))
                at_n5 = sbuf("at_n5_%d_%d" % (m, half), [P, HALF], F32)
                nc.scalar.activation(at_n5[:], s_tiles[m][:].indirect(lists["n5"][:, entries]), ACT.Copy)
                nc.vector.tensor_tensor(result[:, queries], s_tiles[m][:].indirect(lists["n6"][:, entries]), at_n5[:], ALU.mult)
                nc.sync.dma_start(out_rows[m][:, :, queries], result[:, queries])
